import numpy as np
import ml_dtypes


def mxq(x, axis, fmt="e4m3"):
    dtype, down = {"e4m3": (ml_dtypes.float8_e4m3fn, 7), "e5m2": (ml_dtypes.float8_e5m2, 14)}[fmt]
    v = np.moveaxis(np.asarray(x, np.float32).astype(ml_dtypes.bfloat16).astype(np.float64), axis, -1)
    blocks = v.reshape(v.shape[:-1] + (-1, 32))
    amax = np.abs(blocks).max(-1, keepdims=True)
    byte = np.maximum(np.where(amax > 0, np.frexp(amax)[1] - 1 + 127, 0) - down, 1)
    scale = np.exp2(byte - 127.0)
    codes = (blocks / scale).astype(np.float32).astype(dtype).astype(np.float64)
    return np.moveaxis((codes * scale).reshape(v.shape), -1, axis)


WIDE = False


def mx_kscale(k):
    if not WIDE:
        return np.ones(k)
    levels = np.array([10, -10, 5, -5, 0])
    if k % 512:
        return np.exp2(np.random.permutation(np.resize(levels, k // 32))).repeat(32)
    a = np.empty((k // 512, 16))
    for p in range(k // 512):
        a[p, :8] = np.random.permutation(np.resize(levels, 8))
        for g in range(8):
            far = levels[np.abs(levels - a[p, g]) >= 10]
            a[p, g + 8] = far[np.random.randint(len(far))]
    return np.exp2(a.ravel()).repeat(32)


def f64(x):
    return np.asarray(x).astype(np.float64)


def striped(idx):
    return np.tile(idx.reshape(-1, 16).T, (8, 1)).astype(np.uint16)


def unstriped(offs):
    return offs[:16].T.reshape(-1).astype(np.int64)


def pack_weight(w):
    k, n = w.shape
    w = f64(np.asarray(w, np.float32).astype(ml_dtypes.bfloat16)).reshape(k // 32, 32, n)
    amax = np.abs(w).max(1)
    byte = np.clip(np.where(amax > 0, np.frexp(amax)[1] - 1 + 127 - 7, 1), 1, 254)
    scaled = (w * np.exp2(127.0 - byte)[:, None, :]).reshape(k, n).astype(np.float32)
    words = np.ascontiguousarray(scaled.reshape(k // 512, 128, 4, n).transpose(0, 1, 3, 2)).astype(ml_dtypes.float8_e4m3fn).view(np.uint8)
    return words, np.ascontiguousarray(byte.astype(np.uint8).reshape(k // 512, 16, n))


def unpack_weight(words, scales):
    g, p, n, _ = words.shape
    vals = np.ascontiguousarray(words).view(ml_dtypes.float8_e4m3fn).astype(np.float64) * np.repeat(np.exp2(scales.astype(np.float64) - 127.0), 8, axis=1)[..., None]
    return vals.transpose(0, 1, 3, 2).reshape(g * 512, n)


E2M1 = np.array([0.0, 0.5, 1.0, 1.5, 2.0, 3.0, 4.0, 6.0, -0.0, -0.5, -1.0, -1.5, -2.0, -3.0, -4.0, -6.0])


def pack_fp4(w):
    k, n = w.shape
    w = f64(np.asarray(w, np.float32).astype(ml_dtypes.bfloat16)).reshape(k // 32, 32, n)
    amax = np.abs(w).max(1)
    mant, ex = np.frexp(amax / 6.0)
    byte = np.clip(np.where(amax > 0, np.where(mant > 0.5, ex, ex - 1) + 127, 1), 1, 254)
    scaled = (w * np.exp2(127.0 - byte)[:, None, :]).reshape(k, n).astype(np.float32)
    c = np.ascontiguousarray(scaled.reshape(k // 512, 128, 4, n).transpose(0, 1, 3, 2)).astype(ml_dtypes.float4_e2m1fn).view(np.uint8) & 0xF
    words = (c[..., 0::2] | (c[..., 1::2] << 4)).reshape(k // 512, 128, 2 * n)
    return np.ascontiguousarray(words), np.ascontiguousarray(byte.astype(np.uint8).reshape(k // 512, 16, n))


def unpack_fp4(words, scales):
    g, _, n = scales.shape
    words = np.ascontiguousarray(words).reshape(g, 128, n, 2)
    nib = np.empty((g, 128, n, 4), np.uint8)
    nib[..., 0::2] = words & 0xF
    nib[..., 1::2] = words >> 4
    vals = E2M1[nib] * np.repeat(np.exp2(scales.astype(np.float64) - 127.0), 8, axis=1)[..., None]
    return vals.transpose(0, 1, 3, 2).reshape(g * 512, n)


def planes(y):
    n, m = y.shape
    v = y.astype(np.float32).astype(ml_dtypes.bfloat16).astype(np.float64).reshape(n // 32, 32, m)
    top = np.abs(v).max(1)
    byte = np.clip(np.where(top > 0, np.frexp(top)[1] - 1 + 127 - 7, 1), 1, 254)
    codes = (v * np.exp2(127.0 - byte)[:, None, :]).reshape(n, m).astype(np.float32).astype(ml_dtypes.float8_e4m3fn).view(np.uint8)
    words = codes.reshape(n // 512, 128, 4, m).transpose(0, 1, 3, 2)
    return np.ascontiguousarray(words), np.ascontiguousarray(byte.astype(np.uint8).reshape(n // 512, 16, m))


K, T, S, N, H, W = 512, 2048, 512, 512, 512, 256


def setup_inputs():
    n = np.random.standard_normal
    s = mx_kscale(K)[:, None]
    u = mx_kscale(H)
    packed_xT = pack_weight(n((K, T)) * s)
    packed_w1 = pack_fp4(n((K, H)) / np.sqrt(K) / s)
    packed_w2 = pack_fp4(n((H, N)) / np.sqrt(H) / u[:, None])
    perm = np.random.permutation(S)
    return {
        "x_words": packed_xT[0],
        "x_scales": packed_xT[1],
        "w1_words": packed_w1[0],
        "w1_scales": packed_w1[1],
        "gn": (np.random.uniform(0.5, 1.5, (H, 1)) * u[:, None]).astype(np.float32),
        "w2_words": packed_w2[0],
        "w2_scales": packed_w2[1],
        "offs": striped(np.random.permutation(T)[:S]),
        "n1": striped(np.random.permutation(S)),
        "n2": striped(np.random.permutation(S)),
        "n3": striped(perm[:W]),
        "n4": striped(perm[W:]),
    }


def reference(x_words, x_scales, w1_words, w1_scales, gn, w2_words, w2_scales, offs, n1, n2, n3, n4):
    xq = unpack_weight(x_words, x_scales)[:, unstriped(offs)]
    y = unpack_fp4(w1_words, w1_scales).T @ xq
    st = np.maximum(y, y[:, unstriped(n1)])
    z = f64(gn) * (st[:, unstriped(n2)] - (0.5 * y))
    h = unpack_fp4(w2_words, w2_scales).T @ mxq(z, 0, "e4m3")
    pa = h[:, unstriped(n3)]
    pb = h[:, unstriped(n4)]
    rb = np.maximum(pa, pb)
    ra = pa / (np.abs(pb) + 0.5)
    ds = np.zeros((N, S))
    ds[:, unstriped(n3)] = ra
    out = ds.copy()
    out[:, unstriped(n4)] = rb
    return (out,) + planes(out)

@@ -1,0 +1,239 @@
+from contextlib import ExitStack
+
+import concourse.mybir as mybir
+
+K, T, S, N, H, W = 512, 2048, 512, 512, 512, 256
+FLOPS = 2 * K * H * S + 2 * H * N * S
+
+F32 = mybir.dt.float32
+BF16 = mybir.dt.bfloat16
+I32 = mybir.dt.int32
+U32 = mybir.dt.uint32
+U16 = mybir.dt.uint16
+U8 = mybir.dt.uint8
+FP8X4 = mybir.dt.float8_e4m3fn_x4
+FP4X4 = mybir.dt.float4_e2m1fn_x4
+ALU = mybir.AluOpType
+COPY = mybir.ActivationFunctionType.Copy
+
+P = 128
+PACK = 4
+HALF = S // 2
+LIST_HALF = HALF // 16
+
+
+def tile_picked_layhopbratio_none_po_kernel(
+    tc, x_words, x_scales, w1_words, w1_scales, gn, w2_words, w2_scales, offs, n1, n2, n3, n4, out_0, out_1, out_2
+):
+    nc = tc.nc
+    halves = [slice(0, HALF), slice(HALF, S)]
+    list_halves = [slice(0, LIST_HALF), slice(LIST_HALF, 2 * LIST_HALF)]
+
+    with ExitStack() as ctx:
+        lists = ctx.enter_context(tc.tile_pool(name="lists", bufs=1))
+        keep = ctx.enter_context(tc.tile_pool(name="keep", bufs=1))
+        psum = ctx.enter_context(tc.psum_pool(name="psum", bufs=1))
+
+        def load_list(src, name):
+            tile = lists.tile(list(src.shape), U16, name=name)
+            nc.sync.dma_start(tile[:], src)
+            return tile
+
+        def load_scale_rows(tile, src):
+            for q in range(4):
+                nc.sync.dma_start(tile[32 * q : 32 * q + 4, :].bitcast(I32), src[0, 4 * q : 4 * q + 4, :].bitcast(I32))
+
+        def load_words(src, name):
+            tile = keep.tile([P, src.shape[1]], U8, name=name, align_bytes=64)
+            nc.sync.dma_start(tile[:].bitcast(I32), src.bitcast(I32))
+            return tile
+
+        def deal_words(raw, name):
+            tile = keep.tile([P, 2 * H], U8, name=name, align_bytes=64)
+            nc.vector.tensor_copy(
+                out=tile[:].rearrange("p (t m b) -> p t m b", t=PACK, b=2),
+                in_=raw[:].rearrange("p (m t b) -> p t m b", t=PACK, b=2),
+            )
+            return tile
+
+        def deal_scales(tile, raw, ts):
+            nc.vector.tensor_copy(
+                out=tile[:].rearrange("p (t m) -> p t m", t=PACK)[:, ts, :],
+                in_=raw.rearrange("p (m t) -> p t m", t=PACK)[:, ts, :],
+            )
+
+        def product(words, scales, codes, code_scales, t, cols, tag):
+            width = cols.stop - cols.start
+            acc = psum.tile([P, width], F32, name=tag, tag=tag)
+            nc.tensor.matmul_mx(
+                out=acc[:],
+                lhsT=words[:, 2 * P * t : 2 * P * (t + 1)].bitcast(FP4X4),
+                lhsT_scale=scales[:, P * t : P * (t + 1)],
+                rhs=codes[:, cols].bitcast(FP8X4),
+                rhs_scale=code_scales[:, cols],
+                start=True,
+                stop=True,
+            )
+            return acc
+
+        xs_all = keep.tile([P, T], U8, name="xs_all", align_bytes=64)
+        nc.vector.memset(xs_all[:].bitcast(I32), 0)
+        ws_raw = keep.tile([P, H + N], U8, name="ws_raw", align_bytes=64)
+        nc.vector.memset(ws_raw[:].bitcast(I32), 0)
+        offs_t = load_list(offs, "offs_t")
+        w1_raw = load_words(w1_words[0], "w1_raw")
+        w2_raw = load_words(w2_words[0], "w2_raw")
+        load_scale_rows(xs_all, x_scales)
+        xw_all = keep.tile([P, T], I32, name="xw_all", align_bytes=64)
+        nc.sync.dma_start(xw_all[:], x_words[0].rearrange("p c r -> p (c r)").bitcast(I32))
+        load_scale_rows(ws_raw[:, :H], w1_scales)
+        n1_t = load_list(n1, "n1_t")
+        gain = keep.tile([P, PACK], F32, name="gain")
+        nc.sync.dma_start(gain[:], gn.rearrange("(p t) o -> p (t o)", t=PACK))
+        n2_t = load_list(n2, "n2_t")
+        load_scale_rows(ws_raw[:, H:], w2_scales)
+        n4_t = load_list(n4, "n4_t")
+        n3_t = load_list(n3, "n3_t")
+
+        w1 = deal_words(w1_raw, "w1")
+        xs = keep.tile([P, S], U8, name="xs", align_bytes=64)
+        nc.vector.tensor_copy(xs[:], xs_all[:].indirect(offs_t[:]))
+        w2 = deal_words(w2_raw, "w2")
+        xw = keep.tile([P, S], U32, name="xw", align_bytes=64)
+        nc.vector.tensor_copy(xw[:, halves[0]], xw_all[:].bitcast(U32).indirect(offs_t[:, list_halves[0]]))
+        w1s = keep.tile([P, H], U8, name="w1s", align_bytes=64)
+        deal_scales(w1s, ws_raw[:, :H], slice(0, 1))
+        nc.vector.tensor_copy(xw[:, halves[1]], xw_all[:].bitcast(U32).indirect(offs_t[:, list_halves[1]]))
+        deal_scales(w1s, ws_raw[:, :H], slice(1, PACK))
+
+        y = [keep.tile([P, S], F32, name="y%d" % t) for t in range(PACK)]
+        for u in range(2):
+            acc = product(w1, w1s, xw, xs, 0, halves[u], "bank_half%d" % u)
+            nc.scalar.activation(y[0][:, halves[u]], acc[:], COPY)
+        banks = [product(w1, w1s, xw, xs, t, slice(0, S), "bank%d" % t) for t in range(1, PACK)]
+
+        near = {}
+        far = {}
+        st = [keep.tile([P, S], F32, name="st%d" % t) for t in range(PACK)]
+        own = [keep.tile([P, S], F32, name="own%d" % t) for t in range(PACK)]
+        zrows = [keep.tile([P, PACK, HALF], BF16, name="zrows%d" % u) for u in range(2)]
+        zb = [keep.tile([P, HALF, PACK], BF16, name="zb%d" % u, align_bytes=64) for u in range(2)]
+        zq = keep.tile([P, S], U32, name="zq", align_bytes=64)
+        zs = keep.tile([P, S], U8, name="zs", align_bytes=64)
+
+        def leave_bank(t):
+            nc.vector.tensor_copy(y[t][:], banks[t - 1][:])
+
+        def fetch_near(t):
+            near[t] = keep.tile([P, S], F32, name="near%d" % t, tag="near%d" % t)
+            for u in range(2):
+                nc.scalar.activation(near[t][:, halves[u]], y[t][:].indirect(n1_t[:, list_halves[u]]), COPY)
+
+        def larger(t):
+            nc.vector.tensor_tensor(st[t][:], near[t][:], y[t][:], ALU.max)
+
+        def own_share(t):
+            nc.vector.tensor_scalar(own[t][:], y[t][:], gain[:, t : t + 1], 0.5, ALU.mult, ALU.mult)
+
+        def fetch_far(t, u, tag):
+            far[t, u] = keep.tile([P, HALF], F32, name="far%d_%d" % (t, u), tag=tag)
+            nc.scalar.activation(far[t, u][:], st[t][:].indirect(n2_t[:, list_halves[u]]), COPY)
+
+        def difference(t, u):
+            nc.vector.scalar_tensor_tensor(
+                zrows[u][:, t, :], far[t, u][:], gain[:, t : t + 1], own[t][:, halves[u]], ALU.mult, ALU.subtract
+            )
+
+        def weave(pair, u):
+            ts = slice(2 * pair, 2 * pair + 2)
+            nc.vector.tensor_copy(zb[u][:, :, ts], zrows[u][:, ts, :].rearrange("p t c -> p c t"))
+
+        def quantise_z(u):
+            nc.vector.quantize_mx(
+                out=zq[:, halves[u]].bitcast(FP8X4), scales=zs[:, halves[u]], in_=zb[u][:].rearrange("p c t -> p (c t)")
+            )
+
+        leave_bank(1)
+        leave_bank(2)
+        fetch_near(0)
+        fetch_near(1)
+        fetch_near(2)
+        larger(0)
+        leave_bank(3)
+        own_share(0)
+        larger(1)
+        own_share(1)
+        larger(2)
+        own_share(2)
+        own_share(3)
+        fetch_far(0, 0, "far00")
+        fetch_far(0, 1, "far01")
+        fetch_near(3)
+        difference(0, 0)
+        difference(0, 1)
+        w2s = keep.tile([P, N], U8, name="w2s", align_bytes=64)
+        deal_scales(w2s, ws_raw[:, H:], slice(0, PACK))
+        larger(3)
+        for u in range(2):
+            fetch_far(1, u, "far1%d" % u)
+            difference(1, u)
+            weave(0, u)
+        fetch_far(2, 0, "far20")
+        fetch_far(3, 0, "far30")
+        fetch_far(2, 1, "near3")
+        fetch_far(3, 1, "far31")
+        difference(2, 0)
+        difference(3, 0)
+        weave(1, 0)
+        difference(2, 1)
+        quantise_z(0)
+        difference(3, 1)
+        weave(1, 1)
+        quantise_z(1)
+
+        h = [keep.tile([P, S], F32, name="h%d" % t) for t in range(PACK)]
+        for u in range(2):
+            acc = product(w2, w2s, zq, zs, 0, halves[u], "bank_half%d" % u)
+            nc.scalar.activation(h[0][:, halves[u]], acc[:], COPY)
+        for t in range(1, PACK):
+            acc = product(w2, w2s, zq, zs, t, slice(0, S), "bank%d" % t)
+            nc.vector.tensor_copy(h[t][:], acc[:])
+
+        pa = [keep.tile([P, W], F32, name="pa%d" % t) for t in range(PACK)]
+        pb = [keep.tile([P, W], F32, name="pb%d" % t) for t in range(PACK)]
+        ra = [keep.tile([P, W], F32, name="ra%d" % t) for t in range(PACK)]
+        rb = [keep.tile([P, W], F32, name="rb%d" % t) for t in range(PACK)]
+        for t in range(PACK):
+            nc.scalar.activation(pb[t][:], h[t][:].indirect(n4_t[:]), COPY)
+            nc.scalar.activation(pa[t][:], h[t][:].indirect(n3_t[:]), COPY)
+        for t in range(PACK):
+            down = keep.tile([P, W], F32, name="down%d" % t)
+            den = keep.tile([P, W], F32, name="den%d" % t)
+            rec = keep.tile([P, W], F32, name="rec%d" % t)
+            nc.vector.tensor_scalar(down[:], pb[t][:], -1.0, 0.5, ALU.mult, ALU.add)
+            nc.vector.tensor_tensor(rb[t][:], pa[t][:], pb[t][:], ALU.max)
+            nc.vector.scalar_tensor_tensor(den[:], pb[t][:], 0.5, down[:], ALU.add, ALU.max)
+            nc.vector.reciprocal(rec[:], den[:])
+            nc.vector.tensor_tensor(ra[t][:], pa[t][:], rec[:], ALU.mult)
+
+        out_rows = out_0.rearrange("(p t) s -> p t s", t=PACK)
+        ob = [keep.tile([P, HALF, PACK], BF16, name="ob%d" % u, align_bytes=64) for u in range(2)]
+        for t in range(PACK):
+            placed = keep.tile([P, S], F32, name="placed%d" % t)
+            nc.scalar.activation(placed[:].indirect(n4_t[:]), rb[t][:], COPY)
+            nc.scalar.activation(placed[:].indirect(n3_t[:]), ra[t][:], COPY)
+            nc.sync.dma_start(out_rows[:, t, :], placed[:])
+            for u in range(2):
+                nc.vector.tensor_copy(ob[u][:, :, t], placed[:, halves[u]])
+
+        oq = keep.tile([P, S], U32, name="oq", align_bytes=64)
+        osc = keep.tile([P, S], U8, name="osc", align_bytes=64)
+        out_words = out_1[0].rearrange("p c r -> p (c r)").bitcast(I32)
+        for u in range(2):
+            nc.vector.quantize_mx(
+                out=oq[:, halves[u]].bitcast(FP8X4), scales=osc[:, halves[u]], in_=ob[u][:].rearrange("p c t -> p (c t)")
+            )
+            nc.sync.dma_start(out_words[:, halves[u]], oq[:, halves[u]].bitcast(I32))
+        for q in range(4):
+            queue = nc.scalar if q % 2 else nc.sync
+            queue.dma_start(out_2[0, 4 * q : 4 * q + 4, :].bitcast(I32), osc[32 * q : 32 * q + 4, :].bitcast(I32))

@@ -39,9 +39,9 @@ def tile_picked_layhopbratio_none_po_kernel(
             nc.sync.dma_start(tile[:], src)
             return tile
 
-        def load_scale_rows(tile, src):
+        def load_scale_rows(tile, src, queue):
             for q in range(4):
-                nc.sync.dma_start(tile[32 * q : 32 * q + 4, :].bitcast(I32), src[0, 4 * q : 4 * q + 4, :].bitcast(I32))
+                queue.dma_start(tile[32 * q : 32 * q + 4, :].bitcast(I32), src[0, 4 * q : 4 * q + 4, :].bitcast(I32))
 
         def load_words(src, name):
             tile = keep.tile([P, src.shape[1]], U8, name=name, align_bytes=64)
@@ -78,20 +78,22 @@ def tile_picked_layhopbratio_none_po_kernel(
 
         xs_all = keep.tile([P, T], U8, name="xs_all", align_bytes=64)
         nc.vector.memset(xs_all[:].bitcast(I32), 0)
-        ws_raw = keep.tile([P, H + N], U8, name="ws_raw", align_bytes=64)
-        nc.vector.memset(ws_raw[:].bitcast(I32), 0)
+        w1s_raw = keep.tile([P, H], U8, name="w1s_raw", align_bytes=64)
+        nc.vector.memset(w1s_raw[:].bitcast(I32), 0)
+        w2s_raw = keep.tile([P, N], U8, name="w2s_raw", align_bytes=64)
+        nc.vector.memset(w2s_raw[:].bitcast(I32), 0)
         offs_t = load_list(offs, "offs_t")
         w1_raw = load_words(w1_words[0], "w1_raw")
         w2_raw = load_words(w2_words[0], "w2_raw")
-        load_scale_rows(xs_all, x_scales)
+        load_scale_rows(xs_all, x_scales, nc.sync)
         xw_all = keep.tile([P, T], I32, name="xw_all", align_bytes=64)
         nc.sync.dma_start(xw_all[:], x_words[0].rearrange("p c r -> p (c r)").bitcast(I32))
-        load_scale_rows(ws_raw[:, :H], w1_scales)
-        n1_t = load_list(n1, "n1_t")
+        load_scale_rows(w1s_raw, w1_scales, nc.sync)
         gain = keep.tile([P, PACK], F32, name="gain")
-        nc.sync.dma_start(gain[:], gn.rearrange("(p t) o -> p (t o)", t=PACK))
+        nc.gpsimd.dma_start(gain[:], gn.rearrange("(p t) o -> p (t o)", t=PACK))
+        n1_t = load_list(n1, "n1_t")
         n2_t = load_list(n2, "n2_t")
-        load_scale_rows(ws_raw[:, H:], w2_scales)
+        load_scale_rows(w2s_raw, w2_scales, nc.sync)
         n4_t = load_list(n4, "n4_t")
         n3_t = load_list(n3, "n3_t")
 
@@ -102,16 +104,20 @@ def tile_picked_layhopbratio_none_po_kernel(
         xw = keep.tile([P, S], U32, name="xw", align_bytes=64)
         nc.vector.tensor_copy(xw[:, halves[0]], xw_all[:].bitcast(U32).indirect(offs_t[:, list_halves[0]]))
         w1s = keep.tile([P, H], U8, name="w1s", align_bytes=64)
-        deal_scales(w1s, ws_raw[:, :H], slice(0, 1))
+        deal_scales(w1s, w1s_raw[:], slice(0, 1))
         nc.vector.tensor_copy(xw[:, halves[1]], xw_all[:].bitcast(U32).indirect(offs_t[:, list_halves[1]]))
-        deal_scales(w1s, ws_raw[:, :H], slice(1, PACK))
+        deal_scales(w1s, w1s_raw[:], slice(1, PACK))
+        half_gain = keep.tile([P, PACK], F32, name="half_gain")
+        nc.scalar.activation(half_gain[:], gain[:], COPY, scale=0.5)
 
         y = [keep.tile([P, S], F32, name="y%d" % t) for t in range(PACK)]
+        half_banks = [product(w1, w1s, xw, xs, 0, halves[u], "bank_half%d" % u) for u in range(2)]
         for u in range(2):
-            acc = product(w1, w1s, xw, xs, 0, halves[u], "bank_half%d" % u)
-            nc.scalar.activation(y[0][:, halves[u]], acc[:], COPY)
+            nc.scalar.activation(y[0][:, halves[u]], half_banks[u][:], COPY)
         banks = [product(w1, w1s, xw, xs, t, slice(0, S), "bank%d" % t) for t in range(1, PACK)]
 
+        whole = slice(0, HALF)
+        quarters = [slice(0, HALF // 2), slice(HALF // 2, HALF)]
         near = {}
         far = {}
         st = [keep.tile([P, S], F32, name="st%d" % t) for t in range(PACK)]
@@ -130,50 +136,66 @@ def tile_picked_layhopbratio_none_po_kernel(
                 nc.scalar.activation(near[t][:, halves[u]], y[t][:].indirect(n1_t[:, list_halves[u]]), COPY)
 
         def larger(t):
-            nc.vector.tensor_tensor(st[t][:], near[t][:], y[t][:], ALU.max)
+            if t == 0:
+                for u in range(2):
+                    nc.vector.tensor_tensor(st[0][:, halves[u]], near[0][:, halves[u]], half_banks[u][:], ALU.max)
+            else:
+                nc.vector.tensor_tensor(st[t][:], near[t][:], banks[t - 1][:], ALU.max)
 
         def own_share(t):
-            nc.vector.tensor_scalar(own[t][:], y[t][:], gain[:, t : t + 1], 0.5, ALU.mult, ALU.mult)
+            nc.gpsimd.tensor_scalar(own[t][:], y[t][:], half_gain[:, t : t + 1], 0.0, ALU.mult, ALU.add)
 
-        def fetch_far(t, u, tag):
-            far[t, u] = keep.tile([P, HALF], F32, name="far%d_%d" % (t, u), tag=tag)
-            nc.scalar.activation(far[t, u][:], st[t][:].indirect(n2_t[:, list_halves[u]]), COPY)
+        def fetch_far(t, u, tag, part=whole):
+            if part.start == 0:
+                far[t, u] = keep.tile([P, HALF], F32, name="far%d_%d" % (t, u), tag=tag)
+            entries = slice((u * HALF + part.start) // 16, (u * HALF + part.stop) // 16)
+            looked_up = st[t][:].indirect(n2_t[:, entries])
+            if t == 0:
+                nc.vector.tensor_copy(far[t, u][:, part], looked_up)
+            else:
+                nc.scalar.activation(far[t, u][:, part], looked_up, COPY)
 
-        def difference(t, u):
+        def columns(u, part):
+            return slice(u * HALF + part.start, u * HALF + part.stop)
+
+        def difference(t, u, part=whole):
             nc.vector.scalar_tensor_tensor(
-                zrows[u][:, t, :], far[t, u][:], gain[:, t : t + 1], own[t][:, halves[u]], ALU.mult, ALU.subtract
+                zrows[u][:, t, part],
+                far[t, u][:, part],
+                gain[:, t : t + 1],
+                own[t][:, columns(u, part)],
+                ALU.mult,
+                ALU.subtract,
             )
 
-        def weave(pair, u):
+        def weave(pair, u, part=whole):
             ts = slice(2 * pair, 2 * pair + 2)
-            nc.vector.tensor_copy(zb[u][:, :, ts], zrows[u][:, ts, :].rearrange("p t c -> p c t"))
+            nc.vector.tensor_copy(zb[u][:, part, ts], zrows[u][:, ts, part].rearrange("p t c -> p c t"))
 
-        def quantise_z(u):
+        def quantise_z(u, part=whole):
+            cols = columns(u, part)
             nc.vector.quantize_mx(
-                out=zq[:, halves[u]].bitcast(FP8X4), scales=zs[:, halves[u]], in_=zb[u][:].rearrange("p c t -> p (c t)")
+                out=zq[:, cols].bitcast(FP8X4), scales=zs[:, cols], in_=zb[u][:, part, :].rearrange("p c t -> p (c t)")
             )
 
-        leave_bank(1)
-        leave_bank(2)
-        fetch_near(0)
-        fetch_near(1)
-        fetch_near(2)
+        for t in range(1, 3):
+            leave_bank(t)
+        for t in range(3):
+            fetch_near(t)
         larger(0)
         leave_bank(3)
-        own_share(0)
-        larger(1)
-        own_share(1)
-        larger(2)
-        own_share(2)
-        own_share(3)
-        fetch_far(0, 0, "far00")
-        fetch_far(0, 1, "far01")
+        for t in range(PACK):
+            own_share(t)
         fetch_near(3)
+        larger(1)
+        fetch_far(0, 0, "far00")
+        larger(2)
+        fetch_far(0, 1, "far01")
+        larger(3)
         difference(0, 0)
         difference(0, 1)
         w2s = keep.tile([P, N], U8, name="w2s", align_bytes=64)
-        deal_scales(w2s, ws_raw[:, H:], slice(0, PACK))
-        larger(3)
+        deal_scales(w2s, w2s_raw[:], slice(0, PACK))
         for u in range(2):
             fetch_far(1, u, "far1%d" % u)
             difference(1, u)
@@ -181,20 +203,24 @@ def tile_picked_layhopbratio_none_po_kernel(
         fetch_far(2, 0, "far20")
         fetch_far(3, 0, "far30")
         fetch_far(2, 1, "near3")
-        fetch_far(3, 1, "far31")
+        for part in quarters:
+            fetch_far(3, 1, "far31", part)
         difference(2, 0)
         difference(3, 0)
         weave(1, 0)
         difference(2, 1)
         quantise_z(0)
-        difference(3, 1)
-        weave(1, 1)
-        quantise_z(1)
+        for part in quarters:
+            difference(3, 1, part)
+        for part in quarters:
+            weave(1, 1, part)
+        for part in quarters:
+            quantise_z(1, part)
 
         h = [keep.tile([P, S], F32, name="h%d" % t) for t in range(PACK)]
-        for u in range(2):
-            acc = product(w2, w2s, zq, zs, 0, halves[u], "bank_half%d" % u)
-            nc.scalar.activation(h[0][:, halves[u]], acc[:], COPY)
+        for u, cols in enumerate([halves[0]] + [columns(1, part) for part in quarters]):
+            acc = product(w2, w2s, zq, zs, 0, cols, "bank_half%d" % u)
+            nc.scalar.activation(h[0][:, cols], acc[:], COPY)
         for t in range(1, PACK):
             acc = product(w2, w2s, zq, zs, t, slice(0, S), "bank%d" % t)
             nc.vector.tensor_copy(h[t][:], acc[:])

@@ -48,16 +48,14 @@ def tile_picked_layhopbratio_none_po_kernel(
             nc.sync.dma_start(tile[:].bitcast(I32), src.bitcast(I32))
             return tile
 
-        def deal_words(raw, name):
-            tile = keep.tile([P, 2 * H], U8, name=name, align_bytes=64)
-            nc.vector.tensor_copy(
-                out=tile[:].rearrange("p (t m b) -> p t m b", t=PACK, b=2),
-                in_=raw[:].rearrange("p (m t b) -> p t m b", t=PACK, b=2),
+        def deal_words(tile, raw, ts, engine):
+            engine.tensor_copy(
+                out=tile[:].rearrange("p (t m b) -> p t m b", t=PACK, b=2)[:, ts],
+                in_=raw[:].rearrange("p (m t b) -> p t m b", t=PACK, b=2)[:, ts],
             )
-            return tile
 
-        def deal_scales(tile, raw, ts):
-            nc.vector.tensor_copy(
+        def deal_scales(tile, raw, ts, engine=nc.vector):
+            engine.tensor_copy(
                 out=tile[:].rearrange("p (t m) -> p t m", t=PACK)[:, ts, :],
                 in_=raw.rearrange("p (m t) -> p t m", t=PACK)[:, ts, :],
             )
@@ -97,10 +95,12 @@ def tile_picked_layhopbratio_none_po_kernel(
         n4_t = load_list(n4, "n4_t")
         n3_t = load_list(n3, "n3_t")
 
-        w1 = deal_words(w1_raw, "w1")
+        w1 = keep.tile([P, 2 * H], U8, name="w1", align_bytes=64)
+        deal_words(w1, w1_raw, slice(0, PACK), nc.vector)
         xs = keep.tile([P, S], U8, name="xs", align_bytes=64)
         nc.vector.tensor_copy(xs[:], xs_all[:].indirect(offs_t[:]))
-        w2 = deal_words(w2_raw, "w2")
+        w2 = keep.tile([P, 2 * N], U8, name="w2", align_bytes=64)
+        deal_words(w2, w2_raw, slice(0, PACK), nc.vector)
         xw = keep.tile([P, S], U32, name="xw", align_bytes=64)
         nc.vector.tensor_copy(xw[:, halves[0]], xw_all[:].bitcast(U32).indirect(offs_t[:, list_halves[0]]))
         w1s = keep.tile([P, H], U8, name="w1s", align_bytes=64)
@@ -168,9 +168,11 @@ def tile_picked_layhopbratio_none_po_kernel(
                 ALU.subtract,
             )
 
-        def weave(pair, u, part=whole):
-            ts = slice(2 * pair, 2 * pair + 2)
-            nc.vector.tensor_copy(zb[u][:, part, ts], zrows[u][:, ts, part].rearrange("p t c -> p c t"))
+        def weave(u, part=whole):
+            nc.vector.tensor_copy(
+                zb[u][:, part, :].rearrange("p (c i) t -> p c t i", i=4),
+                zrows[u][:, :, part].rearrange("p t (c i) -> p c t i", i=4),
+            )
 
         def quantise_z(u, part=whole):
             cols = columns(u, part)
@@ -178,15 +180,15 @@ def tile_picked_layhopbratio_none_po_kernel(
                 out=zq[:, cols].bitcast(FP8X4), scales=zs[:, cols], in_=zb[u][:, part, :].rearrange("p c t -> p (c t)")
             )
 
-        for t in range(1, 3):
+        for t in range(1, PACK):
             leave_bank(t)
-        for t in range(3):
+        for t in range(PACK):
             fetch_near(t)
         larger(0)
-        leave_bank(3)
+        w2s = keep.tile([P, N], U8, name="w2s", align_bytes=64)
+        deal_scales(w2s, w2s_raw[:], slice(0, PACK), nc.gpsimd)
         for t in range(PACK):
             own_share(t)
-        fetch_near(3)
         larger(1)
         fetch_far(0, 0, "far00")
         larger(2)
@@ -194,12 +196,9 @@ def tile_picked_layhopbratio_none_po_kernel(
         larger(3)
         difference(0, 0)
         difference(0, 1)
-        w2s = keep.tile([P, N], U8, name="w2s", align_bytes=64)
-        deal_scales(w2s, w2s_raw[:], slice(0, PACK))
         for u in range(2):
             fetch_far(1, u, "far1%d" % u)
             difference(1, u)
-            weave(0, u)
         fetch_far(2, 0, "far20")
         fetch_far(3, 0, "far30")
         fetch_far(2, 1, "near3")
@@ -207,13 +206,13 @@ def tile_picked_layhopbratio_none_po_kernel(
             fetch_far(3, 1, "far31", part)
         difference(2, 0)
         difference(3, 0)
-        weave(1, 0)
+        weave(0)
         difference(2, 1)
         quantise_z(0)
         for part in quarters:
             difference(3, 1, part)
         for part in quarters:
-            weave(1, 1, part)
+            weave(1, part)
         for part in quarters:
             quantise_z(1, part)
 

@@ -82,14 +82,14 @@ def tile_picked_layhopbratio_none_po_kernel(
         nc.vector.memset(w2s_raw[:].bitcast(I32), 0)
         offs_t = load_list(offs, "offs_t")
         w1_raw = load_words(w1_words[0], "w1_raw")
-        w2_raw = load_words(w2_words[0], "w2_raw")
+        n1_t = load_list(n1, "n1_t")
         load_scale_rows(xs_all, x_scales, nc.sync)
         xw_all = keep.tile([P, T], I32, name="xw_all", align_bytes=64)
         nc.sync.dma_start(xw_all[:], x_words[0].rearrange("p c r -> p (c r)").bitcast(I32))
         load_scale_rows(w1s_raw, w1_scales, nc.sync)
         gain = keep.tile([P, PACK], F32, name="gain")
         nc.gpsimd.dma_start(gain[:], gn.rearrange("(p t) o -> p (t o)", t=PACK))
-        n1_t = load_list(n1, "n1_t")
+        w2_raw = load_words(w2_words[0], "w2_raw")
         n2_t = load_list(n2, "n2_t")
         load_scale_rows(w2s_raw, w2_scales, nc.sync)
         n4_t = load_list(n4, "n4_t")
@@ -99,21 +99,22 @@ def tile_picked_layhopbratio_none_po_kernel(
         deal_words(w1, w1_raw, slice(0, PACK), nc.vector)
         xs = keep.tile([P, S], U8, name="xs", align_bytes=64)
         nc.vector.tensor_copy(xs[:], xs_all[:].indirect(offs_t[:]))
-        w2 = keep.tile([P, 2 * N], U8, name="w2", align_bytes=64)
-        deal_words(w2, w2_raw, slice(0, PACK), nc.vector)
         xw = keep.tile([P, S], U32, name="xw", align_bytes=64)
         nc.vector.tensor_copy(xw[:, halves[0]], xw_all[:].bitcast(U32).indirect(offs_t[:, list_halves[0]]))
         w1s = keep.tile([P, H], U8, name="w1s", align_bytes=64)
         deal_scales(w1s, w1s_raw[:], slice(0, 1))
         nc.vector.tensor_copy(xw[:, halves[1]], xw_all[:].bitcast(U32).indirect(offs_t[:, list_halves[1]]))
         deal_scales(w1s, w1s_raw[:], slice(1, PACK))
+        w2 = keep.tile([P, 2 * N], U8, name="w2", align_bytes=64)
+        deal_words(w2, w2_raw, slice(0, PACK), nc.vector)
         half_gain = keep.tile([P, PACK], F32, name="half_gain")
         nc.scalar.activation(half_gain[:], gain[:], COPY, scale=0.5)
 
         y = [keep.tile([P, S], F32, name="y%d" % t) for t in range(PACK)]
-        half_banks = [product(w1, w1s, xw, xs, 0, halves[u], "bank_half%d" % u) for u in range(2)]
-        for u in range(2):
-            nc.scalar.activation(y[0][:, halves[u]], half_banks[u][:], COPY)
+        pieces = [halves[0], slice(HALF, HALF + HALF // 2), slice(HALF + HALF // 2, S)]
+        piece_banks = [product(w1, w1s, xw, xs, 0, cols, "bank_half%d" % u) for u, cols in enumerate(pieces)]
+        for cols, bank in zip(pieces, piece_banks):
+            nc.scalar.activation(y[0][:, cols], bank[:], COPY)
         banks = [product(w1, w1s, xw, xs, t, slice(0, S), "bank%d" % t) for t in range(1, PACK)]
 
         whole = slice(0, HALF)
@@ -137,8 +138,8 @@ def tile_picked_layhopbratio_none_po_kernel(
 
         def larger(t):
             if t == 0:
-                for u in range(2):
-                    nc.vector.tensor_tensor(st[0][:, halves[u]], near[0][:, halves[u]], half_banks[u][:], ALU.max)
+                for cols, bank in zip(pieces, piece_banks):
+                    nc.vector.tensor_tensor(st[0][:, cols], near[0][:, cols], bank[:], ALU.max)
             else:
                 nc.vector.tensor_tensor(st[t][:], near[t][:], banks[t - 1][:], ALU.max)
 

from contextlib import ExitStack

import concourse.mybir as mybir

K, T, S, N, H, W = 512, 2048, 512, 512, 512, 256
FLOPS = 2 * K * H * S + 2 * H * N * S

F32 = mybir.dt.float32
BF16 = mybir.dt.bfloat16
I32 = mybir.dt.int32
U32 = mybir.dt.uint32
U16 = mybir.dt.uint16
U8 = mybir.dt.uint8
FP8X4 = mybir.dt.float8_e4m3fn_x4
FP4X4 = mybir.dt.float4_e2m1fn_x4
ALU = mybir.AluOpType
COPY = mybir.ActivationFunctionType.Copy

P = 128
PACK = 4
HALF = S // 2
LIST_HALF = HALF // 16


def tile_picked_layhopbratio_none_po_kernel(
    tc, x_words, x_scales, w1_words, w1_scales, gn, w2_words, w2_scales, offs, n1, n2, n3, n4, out_0, out_1, out_2
):
    nc = tc.nc
    halves = [slice(0, HALF), slice(HALF, S)]
    list_halves = [slice(0, LIST_HALF), slice(LIST_HALF, 2 * LIST_HALF)]

    with ExitStack() as ctx:
        lists = ctx.enter_context(tc.tile_pool(name="lists", bufs=1))
        keep = ctx.enter_context(tc.tile_pool(name="keep", bufs=1))
        psum = ctx.enter_context(tc.psum_pool(name="psum", bufs=1))

        def load_list(src, name):
            tile = lists.tile(list(src.shape), U16, name=name)
            nc.sync.dma_start(tile[:], src)
            return tile

        def load_scale_rows(tile, src, queue):
            for q in range(4):
                queue.dma_start(tile[32 * q : 32 * q + 4, :].bitcast(I32), src[0, 4 * q : 4 * q + 4, :].bitcast(I32))

        def load_words(src, name):
            tile = keep.tile([P, src.shape[1]], U8, name=name, align_bytes=64)
            nc.sync.dma_start(tile[:].bitcast(I32), src.bitcast(I32))
            return tile

        def deal_words(tile, raw, ts, engine):
            engine.tensor_copy(
                out=tile[:].rearrange("p (t m b) -> p t m b", t=PACK, b=2)[:, ts],
                in_=raw[:].rearrange("p (m t b) -> p t m b", t=PACK, b=2)[:, ts],
            )

        def deal_scales(tile, raw, ts, engine=nc.vector):
            engine.tensor_copy(
                out=tile[:].rearrange("p (t m) -> p t m", t=PACK)[:, ts, :],
                in_=raw.rearrange("p (m t) -> p t m", t=PACK)[:, ts, :],
            )

        def product(words, scales, codes, code_scales, t, cols, tag):
            width = cols.stop - cols.start
            acc = psum.tile([P, width], F32, name=tag, tag=tag)
            nc.tensor.matmul_mx(
                out=acc[:],
                lhsT=words[:, 2 * P * t : 2 * P * (t + 1)].bitcast(FP4X4),
                lhsT_scale=scales[:, P * t : P * (t + 1)],
                rhs=codes[:, cols].bitcast(FP8X4),
                rhs_scale=code_scales[:, cols],
                start=True,
                stop=True,
            )
            return acc

        xs_all = keep.tile([P, T], U8, name="xs_all", align_bytes=64)
        nc.vector.memset(xs_all[:].bitcast(I32), 0)
        w1s_raw = keep.tile([P, H], U8, name="w1s_raw", align_bytes=64)
        nc.vector.memset(w1s_raw[:].bitcast(I32), 0)
        w2s_raw = keep.tile([P, N], U8, name="w2s_raw", align_bytes=64)
        nc.vector.memset(w2s_raw[:].bitcast(I32), 0)
        offs_t = load_list(offs, "offs_t")
        w1_raw = load_words(w1_words[0], "w1_raw")
        n1_t = load_list(n1, "n1_t")
        load_scale_rows(xs_all, x_scales, nc.sync)
        xw_all = keep.tile([P, T], I32, name="xw_all", align_bytes=64)
        nc.sync.dma_start(xw_all[:], x_words[0].rearrange("p c r -> p (c r)").bitcast(I32))
        load_scale_rows(w1s_raw, w1_scales, nc.sync)
        gain = keep.tile([P, PACK], F32, name="gain")
        nc.gpsimd.dma_start(gain[:], gn.rearrange("(p t) o -> p (t o)", t=PACK))
        w2_raw = load_words(w2_words[0], "w2_raw")
        n2_t = load_list(n2, "n2_t")
        load_scale_rows(w2s_raw, w2_scales, nc.sync)
        n4_t = load_list(n4, "n4_t")
        n3_t = load_list(n3, "n3_t")

        w1 = keep.tile([P, 2 * H], U8, name="w1", align_bytes=64)
        deal_words(w1, w1_raw, slice(0, PACK), nc.vector)
        xs = keep.tile([P, S], U8, name="xs", align_bytes=64)
        nc.vector.tensor_copy(xs[:], xs_all[:].indirect(offs_t[:]))
        xw = keep.tile([P, S], U32, name="xw", align_bytes=64)
        nc.vector.tensor_copy(xw[:, halves[0]], xw_all[:].bitcast(U32).indirect(offs_t[:, list_halves[0]]))
        w1s = keep.tile([P, H], U8, name="w1s", align_bytes=64)
        deal_scales(w1s, w1s_raw[:], slice(0, 1))
        nc.vector.tensor_copy(xw[:, halves[1]], xw_all[:].bitcast(U32).indirect(offs_t[:, list_halves[1]]))
        deal_scales(w1s, w1s_raw[:], slice(1, PACK))
        w2 = keep.tile([P, 2 * N], U8, name="w2", align_bytes=64)
        deal_words(w2, w2_raw, slice(0, PACK), nc.vector)
        half_gain = keep.tile([P, PACK], F32, name="half_gain")
        nc.scalar.activation(half_gain[:], gain[:], COPY, scale=0.5)

        y = [keep.tile([P, S], F32, name="y%d" % t) for t in range(PACK)]
        pieces = [halves[0], slice(HALF, HALF + HALF // 2), slice(HALF + HALF // 2, S)]
        piece_banks = [product(w1, w1s, xw, xs, 0, cols, "bank_half%d" % u) for u, cols in enumerate(pieces)]
        for cols, bank in zip(pieces, piece_banks):
            nc.scalar.activation(y[0][:, cols], bank[:], COPY)
        banks = [product(w1, w1s, xw, xs, t, slice(0, S), "bank%d" % t) for t in range(1, PACK)]

        whole = slice(0, HALF)
        quarters = [slice(0, HALF // 2), slice(HALF // 2, HALF)]
        near = {}
        far = {}
        st = [keep.tile([P, S], F32, name="st%d" % t) for t in range(PACK)]
        own = [keep.tile([P, S], F32, name="own%d" % t) for t in range(PACK)]
        zrows = [keep.tile([P, PACK, HALF], BF16, name="zrows%d" % u) for u in range(2)]
        zb = [keep.tile([P, HALF, PACK], BF16, name="zb%d" % u, align_bytes=64) for u in range(2)]
        zq = keep.tile([P, S], U32, name="zq", align_bytes=64)
        zs = keep.tile([P, S], U8, name="zs", align_bytes=64)

        def leave_bank(t):
            nc.vector.tensor_copy(y[t][:], banks[t - 1][:])

        def fetch_near(t):
            near[t] = keep.tile([P, S], F32, name="near%d" % t, tag="near%d" % t)
            for u in range(2):
                nc.scalar.activation(near[t][:, halves[u]], y[t][:].indirect(n1_t[:, list_halves[u]]), COPY)

        def larger(t):
            if t == 0:
                for cols, bank in zip(pieces, piece_banks):
                    nc.vector.tensor_tensor(st[0][:, cols], near[0][:, cols], bank[:], ALU.max)
            else:
                nc.vector.tensor_tensor(st[t][:], near[t][:], banks[t - 1][:], ALU.max)

        def own_share(t):
            nc.gpsimd.tensor_scalar(own[t][:], y[t][:], half_gain[:, t : t + 1], 0.0, ALU.mult, ALU.add)

        def fetch_far(t, u, tag, part=whole):
            if part.start == 0:
                far[t, u] = keep.tile([P, HALF], F32, name="far%d_%d" % (t, u), tag=tag)
            entries = slice((u * HALF + part.start) // 16, (u * HALF + part.stop) // 16)
            looked_up = st[t][:].indirect(n2_t[:, entries])
            if t == 0:
                nc.vector.tensor_copy(far[t, u][:, part], looked_up)
            else:
                nc.scalar.activation(far[t, u][:, part], looked_up, COPY)

        def columns(u, part):
            return slice(u * HALF + part.start, u * HALF + part.stop)

        def difference(t, u, part=whole):
            nc.vector.scalar_tensor_tensor(
                zrows[u][:, t, part],
                far[t, u][:, part],
                gain[:, t : t + 1],
                own[t][:, columns(u, part)],
                ALU.mult,
                ALU.subtract,
            )

        def weave(u, part=whole):
            nc.vector.tensor_copy(
                zb[u][:, part, :].rearrange("p (c i) t -> p c t i", i=4),
                zrows[u][:, :, part].rearrange("p t (c i) -> p c t i", i=4),
            )

        def quantise_z(u, part=whole):
            cols = columns(u, part)
            nc.vector.quantize_mx(
                out=zq[:, cols].bitcast(FP8X4), scales=zs[:, cols], in_=zb[u][:, part, :].rearrange("p c t -> p (c t)")
            )

        for t in range(1, PACK):
            leave_bank(t)
        for t in range(PACK):
            fetch_near(t)
        larger(0)
        w2s = keep.tile([P, N], U8, name="w2s", align_bytes=64)
        deal_scales(w2s, w2s_raw[:], slice(0, PACK), nc.gpsimd)
        for t in range(PACK):
            own_share(t)
        larger(1)
        fetch_far(0, 0, "far00")
        larger(2)
        fetch_far(0, 1, "far01")
        larger(3)
        difference(0, 0)
        difference(0, 1)
        for u in range(2):
            fetch_far(1, u, "far1%d" % u)
            difference(1, u)
        fetch_far(2, 0, "far20")
        fetch_far(3, 0, "far30")
        fetch_far(2, 1, "near3")
        for part in quarters:
            fetch_far(3, 1, "far31", part)
        difference(2, 0)
        difference(3, 0)
        weave(0)
        difference(2, 1)
        quantise_z(0)
        for part in quarters:
            difference(3, 1, part)
        for part in quarters:
            weave(1, part)
        for part in quarters:
            quantise_z(1, part)

        h = [keep.tile([P, S], F32, name="h%d" % t) for t in range(PACK)]
        for u, cols in enumerate([halves[0]] + [columns(1, part) for part in quarters]):
            acc = product(w2, w2s, zq, zs, 0, cols, "bank_half%d" % u)
            nc.scalar.activation(h[0][:, cols], acc[:], COPY)
        for t in range(1, PACK):
            acc = product(w2, w2s, zq, zs, t, slice(0, S), "bank%d" % t)
            nc.vector.tensor_copy(h[t][:], acc[:])

        pa = [keep.tile([P, W], F32, name="pa%d" % t) for t in range(PACK)]
        pb = [keep.tile([P, W], F32, name="pb%d" % t) for t in range(PACK)]
        ra = [keep.tile([P, W], F32, name="ra%d" % t) for t in range(PACK)]
        rb = [keep.tile([P, W], F32, name="rb%d" % t) for t in range(PACK)]
        for t in range(PACK):
            nc.scalar.activation(pb[t][:], h[t][:].indirect(n4_t[:]), COPY)
            nc.scalar.activation(pa[t][:], h[t][:].indirect(n3_t[:]), COPY)
        for t in range(PACK):
            down = keep.tile([P, W], F32, name="down%d" % t)
            den = keep.tile([P, W], F32, name="den%d" % t)
            rec = keep.tile([P, W], F32, name="rec%d" % t)
            nc.vector.tensor_scalar(down[:], pb[t][:], -1.0, 0.5, ALU.mult, ALU.add)
            nc.vector.tensor_tensor(rb[t][:], pa[t][:], pb[t][:], ALU.max)
            nc.vector.scalar_tensor_tensor(den[:], pb[t][:], 0.5, down[:], ALU.add, ALU.max)
            nc.vector.reciprocal(rec[:], den[:])
            nc.vector.tensor_tensor(ra[t][:], pa[t][:], rec[:], ALU.mult)

        out_rows = out_0.rearrange("(p t) s -> p t s", t=PACK)
        ob = [keep.tile([P, HALF, PACK], BF16, name="ob%d" % u, align_bytes=64) for u in range(2)]
        for t in range(PACK):
            placed = keep.tile([P, S], F32, name="placed%d" % t)
            nc.scalar.activation(placed[:].indirect(n4_t[:]), rb[t][:], COPY)
            nc.scalar.activation(placed[:].indirect(n3_t[:]), ra[t][:], COPY)
            nc.sync.dma_start(out_rows[:, t, :], placed[:])
            for u in range(2):
                nc.vector.tensor_copy(ob[u][:, :, t], placed[:, halves[u]])

        oq = keep.tile([P, S], U32, name="oq", align_bytes=64)
        osc = keep.tile([P, S], U8, name="osc", align_bytes=64)
        out_words = out_1[0].rearrange("p c r -> p (c r)").bitcast(I32)
        for u in range(2):
            nc.vector.quantize_mx(
                out=oq[:, halves[u]].bitcast(FP8X4), scales=osc[:, halves[u]], in_=ob[u][:].rearrange("p c t -> p (c t)")
            )
            nc.sync.dma_start(out_words[:, halves[u]], oq[:, halves[u]].bitcast(I32))
        for q in range(4):
            queue = nc.scalar if q % 2 else nc.sync
            queue.dma_start(out_2[0, 4 * q : 4 * q + 4, :].bitcast(I32), osc[32 * q : 32 * q + 4, :].bitcast(I32))
